import numpy as np
import ml_dtypes


def mxq(x, axis, fmt="e4m3"):
    dtype, down = {"e4m3": (ml_dtypes.float8_e4m3fn, 7), "e5m2": (ml_dtypes.float8_e5m2, 14)}[fmt]
    v = np.moveaxis(np.asarray(x, np.float32).astype(ml_dtypes.bfloat16).astype(np.float64), axis, -1)
    blocks = v.reshape(v.shape[:-1] + (-1, 32))
    amax = np.abs(blocks).max(-1, keepdims=True)
    byte = np.maximum(np.where(amax > 0, np.frexp(amax)[1] - 1 + 127, 0) - down, 1)
    scale = np.exp2(byte - 127.0)
    codes = (blocks / scale).astype(np.float32).astype(dtype).astype(np.float64)
    return np.moveaxis((codes * scale).reshape(v.shape), -1, axis)


WIDE = False


def mx_kscale(k):
    if not WIDE:
        return np.ones(k)
    levels = np.array([10, -10, 5, -5, 0])
    if k % 512:
        return np.exp2(np.random.permutation(np.resize(levels, k // 32))).repeat(32)
    a = np.empty((k // 512, 16))
    for p in range(k // 512):
        a[p, :8] = np.random.permutation(np.resize(levels, 8))
        for g in range(8):
            far = levels[np.abs(levels - a[p, g]) >= 10]
            a[p, g + 8] = far[np.random.randint(len(far))]
    return np.exp2(a.ravel()).repeat(32)


BF16 = ml_dtypes.bfloat16


def bf(x):
    return np.asarray(x, np.float32).astype(BF16)


def f64(x):
    return np.asarray(x).astype(np.float64)


E2M1 = np.array([0.0, 0.5, 1.0, 1.5, 2.0, 3.0, 4.0, 6.0, -0.0, -0.5, -1.0, -1.5, -2.0, -3.0, -4.0, -6.0])


def pack_weight(w, fmt):
    k, n = w.shape
    w = f64(bf(w)).reshape(k // 32, 32, n)
    amax = np.abs(w).max(1)
    if fmt == "e4m3":
        byte = np.frexp(amax)[1] - 1 + 127 - 7
    else:
        mant, ex = np.frexp(amax / 6.0)
        byte = np.where(mant > 0.5, ex, ex - 1) + 127
    byte = np.clip(np.where(amax > 0, byte, 1), 1, 254)
    scaled = (w * np.exp2(127.0 - byte)[:, None, :]).reshape(k, n).astype(np.float32)
    by_word = np.ascontiguousarray(scaled.reshape(k // 512, 128, 4, n).transpose(0, 1, 3, 2))
    if fmt == "e4m3":
        words = by_word.astype(ml_dtypes.float8_e4m3fn).view(np.uint8)
    else:
        c = by_word.astype(ml_dtypes.float4_e2m1fn).view(np.uint8) & 0xF
        words = c[..., 0::2] | (c[..., 1::2] << 4)
    return np.ascontiguousarray(words), np.ascontiguousarray(byte.astype(np.uint8).reshape(k // 512, 16, n))


def unpack_weight(words, scales, fmt):
    g, p, n, _ = words.shape
    if fmt == "e4m3":
        vals = np.ascontiguousarray(words).view(ml_dtypes.float8_e4m3fn).astype(np.float64)
    else:
        nib = np.empty((g, p, n, 4), np.uint8)
        nib[..., 0::2] = words & 0xF
        nib[..., 1::2] = words >> 4
        vals = E2M1[nib]
    vals = vals * np.repeat(np.exp2(scales.astype(np.float64) - 127.0), 8, axis=1)[..., None]
    return vals.transpose(0, 1, 3, 2).reshape(g * 512, n)
def pack4(w):
    words, scales = pack_weight(w, "e2m1")
    return words.reshape(words.shape[0], 128, -1), scales


def unpack4(words, scales):
    return unpack_weight(words.reshape(words.shape[0], 128, -1, 2), scales, "e2m1")


B, S, E, D = 2, 512, 1024, 512
SLOPE = 0.1


def leaky(z):
    return np.maximum(z, SLOPE * z)


def draw0():
    sd, se, t = mx_kscale(D), mx_kscale(E), mx_kscale(D)
    d = bf(np.random.standard_normal((B, S, D)) * sd)
    e = bf(np.random.standard_normal((B, S, E)) * se)
    u_mat_words, u_mat_scales = pack4(np.random.standard_normal((D, D)) * (2.0 / np.sqrt(D)) / sd[:, None] / t[None, :])
    u_vec = bf(np.random.standard_normal(D) / t)
    wh_words, wh_scales = pack4(np.random.standard_normal((E, D)) / np.sqrt(E) / se[:, None] * t[None, :])
    bh = bf(np.random.standard_normal(D) * 0.5 * t)
    return {"d": d,
            "e": e,
            "u_mat_words": u_mat_words,
            "u_mat_scales": u_mat_scales,
            "u_vec": u_vec,
            "wh_words": wh_words,
            "wh_scales": wh_scales,
            "bh": bh}


def core(d, e, u_mat_words, u_mat_scales, u_vec, wh_words, wh_scales, bh):
    q = (mxq(f64(d), 2, "e4m3") @ unpack4(u_mat_words, u_mat_scales)) + f64(u_vec)
    z = (mxq(f64(e), 2, "e4m3") @ unpack4(wh_words, wh_scales)) + f64(bh)
    h = leaky(z)
    s = (mxq(q, 2, "e4m3") @ mxq(h, 2, "e4m3").transpose(0, 2, 1)) / np.sqrt(D)
    m = s.max(axis=-1, keepdims=True)
    return s - (m + np.log(np.sum(np.exp(s - m), axis=-1, keepdims=True)))


def e4m3fn_bytes(y):
    return np.clip(np.asarray(y, np.float64), -448.0, 448.0).astype(np.float32).astype(ml_dtypes.float8_e4m3fn).view(np.uint8)


def e4m3fn_values(b):
    return np.asarray(b, np.uint8).view(ml_dtypes.float8_e4m3fn).astype(np.float64)


def setup_inputs():
    d = draw0()
    x0 = np.asarray(d['e']).astype(np.float64)
    s = (np.max(np.abs(x0), axis=(0, 1), keepdims=True) / 448.0).astype(np.float32)
    out = {}
    for k, v in d.items():
        if k == 'e':
            out['e_bytes'] = e4m3fn_bytes(x0 / s.astype(np.float64))
            out['e_scale'] = s
        else:
            out[k] = v
    return out


def reference(d, e_bytes, e_scale, u_mat_words, u_mat_scales, u_vec, wh_words, wh_scales, bh):
    return core(d, e4m3fn_values(e_bytes) * e_scale.astype(np.float64), u_mat_words, u_mat_scales, u_vec, wh_words, wh_scales, bh)

@@ -1,0 +1,402 @@
+import math
+from contextlib import ExitStack
+
+import concourse.mybir as mybir
+from concourse.masks import make_identity
+
+B, S, E, D = 2, 512, 1024, 512
+SLOPE = 0.1
+FLOPS = 2 * B * S * (D * D + E * D + S * D)
+
+F32 = mybir.dt.float32
+BF16 = mybir.dt.bfloat16
+I32 = mybir.dt.int32
+U32 = mybir.dt.uint32
+U8 = mybir.dt.uint8
+FP8 = mybir.dt.float8_e4m3fn
+FP8X4 = mybir.dt.float8_e4m3fn_x4
+FP4X4 = mybir.dt.float4_e2m1fn_x4
+ALU = mybir.AluOpType
+ACT = mybir.ActivationFunctionType
+
+P = 128
+TILES = S // P
+E_PASSES = E // 512
+
+
+def tile_biaffinearclogprobabilities_w4_kernel(
+    tc, d, e_bytes, e_scale, u_mat_words, u_mat_scales, u_vec, wh_words, wh_scales, bh, out
+):
+    nc = tc.nc
+    with ExitStack() as ctx:
+        sb = ctx.enter_context(tc.tile_pool(name="sb", bufs=1))
+        ps = ctx.enter_context(tc.psum_pool(name="ps", bufs=8))
+        ctx.enter_context(tc.manual_schedule())
+
+        def keep(name, shape, dtype):
+            return sb.tile(shape, dtype, name=name, tag=name, align_bytes=64)
+
+        def bank(name, shape, dtype):
+            return ps.tile(shape, dtype, name=name, tag="bank")
+
+        ident32 = keep("ident32", [P, P], F32)
+        ident16 = keep("ident16", [P, P], BF16)
+        scale_col = keep("scale_col", [P, E_PASSES, 4], F32)
+        scale_all = keep("scale_all", [P, E], F32)
+        e_raw = [keep("e_raw%d" % n, [P, 2, E], U8) for n in range(B * TILES // 2)]
+        e_bf = [keep("e_bf%d" % n, [P, E], BF16) for n in range(B * TILES)]
+        e_grp = [keep("e_grp%d" % b, [P, E_PASSES, S, 2], F32) for b in range(B)]
+        e_codes = [keep("e_codes%d" % b, [P, E_PASSES, S], U32) for b in range(B)]
+        e_scl = [keep("e_scl%d" % b, [P, E_PASSES, S], U8) for b in range(B)]
+        d_raw = [keep("d_raw%d" % b, [P, TILES, D], BF16) for b in range(B)]
+        d_grp = [keep("d_grp%d" % b, [P, S, 2], F32) for b in range(B)]
+        d_codes = [keep("d_codes%d" % b, [P, S], U32) for b in range(B)]
+        d_scl = [keep("d_scl%d" % b, [P, S], U8) for b in range(B)]
+        uw_raw = keep("uw_raw", [P, 1, 2 * D], U8)
+        ww_raw = keep("ww_raw", [P, E_PASSES, 2 * D], U8)
+        us_raw = keep("us_raw", [P, 1, D], U8)
+        ws_raw = keep("ws_raw", [P, E_PASSES, D], U8)
+        uw = keep("uw", [P, 1, 2 * D], U8)
+        ww = keep("ww", [P, E_PASSES, 2 * D], U8)
+        us = keep("us", [P, 1, D], U8)
+        ws = keep("ws", [P, E_PASSES, D], U8)
+        bias_rows = keep("bias_rows", [P, P], BF16)
+        bias = keep("bias", [P, 8], F32)
+        x_planes = [keep("x_planes%d" % b, [P, 4, S], F32) for b in range(B)]
+        h_grp = [keep("h_grp%d" % b, [P, S, 4], BF16) for b in range(B)]
+        h_codes = [keep("h_codes%d" % b, [P, S], U32) for b in range(B)]
+        h_scl = [keep("h_scl%d" % b, [P, S], U8) for b in range(B)]
+        q_grp = [keep("q_grp%d" % b, [P, S, 4], BF16) for b in range(B)]
+        q_codes = [keep("q_codes%d" % b, [P, S], U32) for b in range(B)]
+        q_scl = [keep("q_scl%d" % b, [P, S], U8) for b in range(B)]
+        neg_s = [keep("neg_s%d" % n, [P, S], F32) for n in range(B * TILES)]
+        res = [keep("res%d" % n, [P, S], F32) for n in range(B * TILES)]
+        exp_out = keep("exp_out", [P, S], BF16)
+        neg_max = [keep("neg_max%d" % b, [P, TILES], F32) for b in range(B)]
+        sums = [keep("sums%d" % b, [P, TILES], F32) for b in range(B)]
+        q_planes = [keep("q_planes%d" % b, [P, 4, S], BF16) for b in range(B)]
+        logs = [keep("logs%d" % b, [P, TILES], F32) for b in range(B)]
+        shift = [keep("shift%d" % b, [P, TILES], F32) for b in range(B)]
+        banks = {}
+
+        make_identity(nc, ident32[:])
+        nc.vector.memset(bias_rows[:], 0.0)
+        nc.vector.memset(us_raw[:].bitcast(I32), 0)
+        nc.vector.memset(ws_raw[:].bitcast(I32), 0)
+        nc.scalar.activation(out=ident16[:], in_=ident32[:], func=ACT.Copy)
+
+        def load_e(n):
+            b, half = divmod(n, 2)
+            rows = e_bytes[b, 256 * half : 256 * half + 256, :]
+            nc.sync.dma_start(out=e_raw[n][:], in_=rows.rearrange("(j p) k -> p j k", p=P))
+
+        def load_d(b):
+            nc.sync.dma_start(out=d_raw[b][:], in_=d[b].rearrange("(p j) k -> p j k", j=TILES))
+
+        nc.sync.dma_start(out=scale_col[:], in_=e_scale.rearrange("a o (g p c) -> p (a o g) c", g=E_PASSES, c=4))
+        def load_words(raw, src):
+            nc.sync.dma_start(out=raw[:].bitcast(I32), in_=src.bitcast(I32).rearrange("g p w -> p g w"))
+
+        def load_scales(raw, src):
+            for quad in range(4):
+                nc.sync.dma_start(
+                    out=raw[32 * quad : 32 * quad + 4, :, :].bitcast(I32),
+                    in_=src.bitcast(I32)[:, 4 * quad : 4 * quad + 4, :].rearrange("g r w -> r g w"),
+                )
+
+        def load_bias(row, vec):
+            nc.sync.dma_start(
+                out=bias_rows[row : row + 4, :].rearrange("t (j r) -> t j r", r=8),
+                in_=vec.rearrange("(j t r) -> t j r", t=4, r=8),
+            )
+
+        load_words(uw_raw, u_mat_words)
+        load_words(ww_raw, wh_words)
+        load_e(0)
+        load_e(1)
+        load_d(0)
+        load_e(2)
+        load_bias(0, u_vec)
+        load_bias(4, bh)
+        load_scales(us_raw, u_mat_scales)
+        load_scales(ws_raw, wh_scales)
+        load_e(3)
+        load_d(1)
+
+        def spread_scale(g, copy):
+            acc = bank("spread", [P, 4, P], F32)
+            for c in range(4):
+                nc.tensor.transpose(acc[:, c, :], scale_col[:, g, c : c + 1].to_broadcast([P, P]), ident32[:])
+            dst = scale_all[:, 512 * g : 512 * g + 512].rearrange("p (n c) -> p n c", c=4)
+            copy(out=dst, in_=acc[:].rearrange("p c n -> p n c"))
+
+        def scale_e(n):
+            nc.vector.tensor_tensor(
+                out=e_bf[n][:], in0=e_raw[n // 2][:, n % 2, :].bitcast(FP8), in1=scale_all[:], op=ALU.mult
+            )
+
+        def turn_e(n):
+            b, j = divmod(n, TILES)
+            acc = bank("turn_e", [P, E_PASSES, 2, P], F32)
+            words = e_bf[n][:].bitcast(F32)
+            for g in range(E_PASSES):
+                for u in range(2):
+                    nc.tensor.transpose(acc[:, g, u, :], words[:, 256 * g + u : 256 * g + 256 : 2], ident32[:])
+            nc.scalar.copy(out=e_grp[b][:, :, P * j : P * j + P, :], in_=acc[:].rearrange("p g u r -> p g r u"))
+
+        def turn_d(b, half):
+            acc = bank("turn_d", [P, 2, 2, P], F32)
+            for jj in range(2):
+                words = d_raw[b][:, 2 * half + jj, :].bitcast(F32)
+                for u in range(2):
+                    nc.tensor.transpose(acc[:, jj, u, :], words[:, u:256:2], ident32[:])
+            dst = d_grp[b][:, 256 * half : 256 * half + 256, :].rearrange("p (j r) u -> p j r u", j=2)
+            nc.scalar.copy(out=dst, in_=acc[:].rearrange("p j u r -> p j r u"))
+
+        def turn_bias():
+            acc = bank("turn_bias", [P, P], BF16)
+            nc.tensor.transpose(acc[:], bias_rows[:], ident16[:])
+            nc.scalar.copy(out=bias[:], in_=acc[:, 0:8])
+
+        def reorder(dst, src):
+            nc.vector.tensor_copy(
+                out=dst[:].bitcast(I32).rearrange("p g (t j w) -> p g t j w", t=4, j=16),
+                in_=src[:].bitcast(I32).rearrange("p g (j t w) -> p g t j w", t=4, j=16),
+            )
+
+        def quantize(codes, scales, values):
+            nc.vector.quantize_mx(out=codes.bitcast(FP8X4), scales=scales, in_=values)
+
+        def quant_e(b, g):
+            values = e_grp[b][:, g, :, :].rearrange("p r u -> p (r u)").bitcast(BF16)
+            quantize(e_codes[b][:, g, :], e_scl[b][:, g, :], values)
+
+        def quant_d(b):
+            quantize(d_codes[b][:], d_scl[b][:], d_grp[b][:].rearrange("p r u -> p (r u)").bitcast(BF16))
+
+        def quant_h(b):
+            quantize(h_codes[b][:], h_scl[b][:], h_grp[b][:].rearrange("p n t -> p (n t)"))
+
+        def quant_q(b, half):
+            cols = slice(256 * half, 256 * half + 256)
+            quantize(q_codes[b][:, cols], q_scl[b][:, cols], q_grp[b][:, cols, :].rearrange("p n t -> p (n t)"))
+
+        def z_plane(b, t):
+            acc = bank("z", [P, S], F32)
+            for g in range(E_PASSES):
+                nc.tensor.matmul_mx(
+                    out=acc[:],
+                    lhsT=ww[:, g, 256 * t : 256 * t + 256].bitcast(FP4X4),
+                    lhsT_scale=ws[:, g, P * t : P * t + P],
+                    rhs=e_codes[b][:, g, :].bitcast(FP8X4),
+                    rhs_scale=e_scl[b][:, g, :],
+                    start=(g == 0),
+                    stop=(g == E_PASSES - 1),
+                )
+            nc.scalar.activation(
+                out=x_planes[b][:, t, :], in_=acc[:], func=ACT.Identity, bias=bias[:, 4 + t : 5 + t], scale=1.0
+            )
+
+        def leaky(b, half):
+            cols = slice(256 * half, 256 * half + 256)
+            x = x_planes[b][:, :, cols].rearrange("p t n -> p n t")
+            nc.vector.scalar_tensor_tensor(
+                out=h_grp[b][:, cols, :], in0=x, scalar=SLOPE, in1=x, op0=ALU.mult, op1=ALU.max
+            )
+
+        def q_plane(b, t):
+            acc = bank("q", [P, S], F32)
+            nc.tensor.matmul_mx(
+                out=acc[:],
+                lhsT=uw[:, 0, 256 * t : 256 * t + 256].bitcast(FP4X4),
+                lhsT_scale=us[:, 0, P * t : P * t + P],
+                rhs=d_codes[b][:].bitcast(FP8X4),
+                rhs_scale=d_scl[b][:],
+                start=True,
+                stop=True,
+            )
+            nc.scalar.activation(
+                out=q_planes[b][:, t, :], in_=acc[:], func=ACT.Identity, bias=bias[:, t : t + 1], scale=1.0
+            )
+
+        def q_weave(b, half):
+            cols = slice(256 * half, 256 * half + 256)
+            nc.vector.tensor_copy(
+                out=q_grp[b][:, cols, :].rearrange("p (c i) t -> p c t i", i=4),
+                in_=q_planes[b][:, :, cols].rearrange("p t (c i) -> p c t i", i=4),
+            )
+
+        def leaky4(b, quarter):
+            cols = slice(P * quarter, P * quarter + P)
+            x = x_planes[b][:, :, cols].rearrange("p t n -> p n t")
+            nc.vector.scalar_tensor_tensor(
+                out=h_grp[b][:, cols, :], in0=x, scalar=SLOPE, in1=x, op0=ALU.mult, op1=ALU.max
+            )
+
+        def scale_e_half(n, g):
+            cols = slice(512 * g, 512 * g + 512)
+            nc.vector.tensor_tensor(
+                out=e_bf[n][:, cols],
+                in0=e_raw[n // 2][:, n % 2, cols].bitcast(FP8),
+                in1=scale_all[:, cols],
+                op=ALU.mult,
+            )
+
+        def s_matmul(b, i):
+            acc = bank("s", [P, S], F32)
+            banks[("s", b, i)] = acc
+            cols = slice(P * i, P * i + P)
+            nc.tensor.matmul_mx(
+                out=acc[:],
+                lhsT=q_codes[b][:, cols].bitcast(FP8X4),
+                lhsT_scale=q_scl[b][:, cols],
+                rhs=h_codes[b][:].bitcast(FP8X4),
+                rhs_scale=h_scl[b][:],
+                start=True,
+                stop=True,
+            )
+
+        def row_max(b, i):
+            nc.vector.tensor_scalar(
+                out=neg_s[TILES * b + i][:],
+                in0=banks[("s", b, i)][:],
+                scalar1=-1.0 / math.sqrt(D),
+                scalar2=None,
+                op0=ALU.mult,
+                op1=ALU.min,
+                accum_out=neg_max[b][:, i : i + 1],
+            )
+
+        def row_sum(b, i):
+            nc.scalar.activation(
+                out=exp_out[:],
+                in_=neg_s[TILES * b + i][:],
+                func=ACT.Exp,
+                bias=neg_max[b][:, i : i + 1],
+                scale=-1.0,
+                accum_out=sums[b][:, i : i + 1],
+            )
+
+        def row_log(b):
+            nc.scalar.activation(out=logs[b][:], in_=sums[b][:], func=ACT.Ln)
+
+        def row_shift(b):
+            nc.vector.tensor_tensor(out=shift[b][:], in0=neg_max[b][:], in1=logs[b][:], op=ALU.subtract)
+
+        def store(b, i):
+            nc.sync.dma_start(out=out[b].rearrange("(p j) n -> j p n", j=TILES)[i], in_=res[TILES * b + i][:])
+
+        def finish_on_scalar(b, i):
+            n = TILES * b + i
+            nc.scalar.activation(
+                out=res[n][:], in_=neg_s[n][:], func=ACT.Identity, bias=shift[b][:, i : i + 1], scale=-1.0
+            )
+            store(b, i)
+
+        def finish_on_vector(b, i):
+            n = TILES * b + i
+            nc.vector.tensor_scalar(
+                out=res[n][:], in0=neg_s[n][:], scalar1=-1.0, scalar2=shift[b][:, i : i + 1], op0=ALU.mult, op1=ALU.add
+            )
+            store(b, i)
+
+        reorder(uw, uw_raw)
+        reorder(ww, ww_raw)
+        spread_scale(0, nc.scalar.copy)
+        spread_scale(1, nc.scalar.copy)
+        scale_e_half(0, 0)
+        scale_e_half(0, 1)
+        scale_e(1)
+        turn_e(0)
+        turn_d(0, 0)
+        turn_d(0, 1)
+        scale_e(2)
+        turn_e(1)
+        turn_bias()
+        scale_e(3)
+        turn_e(2)
+        quant_d(0)
+        reorder(us, us_raw)
+        scale_e(4)
+        turn_e(3)
+        q_plane(0, 0)
+        q_plane(0, 1)
+        reorder(ws, ws_raw)
+        quant_e(0, 0)
+        q_plane(0, 2)
+        q_plane(0, 3)
+        turn_e(4)
+        quant_e(0, 1)
+        scale_e(5)
+        z_plane(0, 0)
+        z_plane(0, 1)
+        turn_e(5)
+        q_weave(0, 0)
+        scale_e(6)
+        turn_d(1, 0)
+        turn_d(1, 1)
+        z_plane(0, 2)
+        z_plane(0, 3)
+        turn_e(6)
+        scale_e(7)
+        turn_e(7)
+        q_weave(0, 1)
+        quant_d(1)
+        q_plane(1, 0)
+        q_plane(1, 1)
+        q_plane(1, 2)
+        q_plane(1, 3)
+        leaky(0, 0)
+        quant_e(1, 0)
+        quant_e(1, 1)
+        z_plane(1, 0)
+        z_plane(1, 1)
+        leaky(0, 1)
+        quant_q(0, 0)
+        quant_h(0)
+        z_plane(1, 2)
+        z_plane(1, 3)
+        s_matmul(0, 0)
+        s_matmul(0, 1)
+        quant_q(0, 1)
+        s_matmul(0, 2)
+        s_matmul(0, 3)
+        q_weave(1, 0)
+        row_max(0, 0)
+        row_sum(0, 0)
+        row_max(0, 1)
+        row_sum(0, 1)
+        row_max(0, 2)
+        row_sum(0, 2)
+        row_max(0, 3)
+        row_sum(0, 3)
+        row_log(0)
+        leaky(1, 0)
+        leaky(1, 1)
+        quant_q(1, 0)
+        quant_h(1)
+        s_matmul(1, 0)
+        s_matmul(1, 1)
+        q_weave(1, 1)
+        row_max(1, 0)
+        row_sum(1, 0)
+        quant_q(1, 1)
+        s_matmul(1, 2)
+        s_matmul(1, 3)
+        row_max(1, 1)
+        row_sum(1, 1)
+        row_max(1, 2)
+        row_sum(1, 2)
+        row_max(1, 3)
+        row_sum(1, 3)
+        row_log(1)
+        row_shift(0)
+        finish_on_vector(0, 0)
+        finish_on_vector(0, 1)
+        finish_on_vector(0, 2)
+        finish_on_vector(0, 3)
+        row_shift(1)
+        finish_on_vector(1, 0)
+        finish_on_vector(1, 1)
+        finish_on_scalar(1, 3)
+        finish_on_vector(1, 2)

@@ -43,7 +43,9 @@ def tile_biaffinearclogprobabilities_w4_kernel(
         ident16 = keep("ident16", [P, P], BF16)
         scale_col = keep("scale_col", [P, E_PASSES, 4], F32)
         scale_all = keep("scale_all", [P, E], F32)
-        e_raw = [keep("e_raw%d" % n, [P, 2, E], U8) for n in range(B * TILES // 2)]
+        e_loads = ((0, 1), (1, 4), (4, 8))
+        e_raw = [keep("e_raw%d" % lo, [P, hi - lo, E], U8) for lo, hi in e_loads]
+        e_tile = [e_raw[m][:, n - lo, :] for m, (lo, hi) in enumerate(e_loads) for n in range(lo, hi)]
         e_bf = [keep("e_bf%d" % n, [P, E], BF16) for n in range(B * TILES)]
         e_grp = [keep("e_grp%d" % b, [P, E_PASSES, S, 2], F32) for b in range(B)]
         e_codes = [keep("e_codes%d" % b, [P, E_PASSES, S], U32) for b in range(B)]
@@ -71,7 +73,7 @@ def tile_biaffinearclogprobabilities_w4_kernel(
         q_scl = [keep("q_scl%d" % b, [P, S], U8) for b in range(B)]
         neg_s = [keep("neg_s%d" % n, [P, S], F32) for n in range(B * TILES)]
         res = [keep("res%d" % n, [P, S], F32) for n in range(B * TILES)]
-        exp_out = keep("exp_out", [P, S], BF16)
+        exp_out = [keep("exp_out%d" % n, [P, S], BF16) for n in range(2)]
         neg_max = [keep("neg_max%d" % b, [P, TILES], F32) for b in range(B)]
         sums = [keep("sums%d" % b, [P, TILES], F32) for b in range(B)]
         q_planes = [keep("q_planes%d" % b, [P, 4, S], BF16) for b in range(B)]
@@ -85,10 +87,10 @@ def tile_biaffinearclogprobabilities_w4_kernel(
         nc.vector.memset(ws_raw[:].bitcast(I32), 0)
         nc.scalar.activation(out=ident16[:], in_=ident32[:], func=ACT.Copy)
 
-        def load_e(n):
-            b, half = divmod(n, 2)
-            rows = e_bytes[b, 256 * half : 256 * half + 256, :]
-            nc.sync.dma_start(out=e_raw[n][:], in_=rows.rearrange("(j p) k -> p j k", p=P))
+        def load_e(m):
+            lo, hi = e_loads[m]
+            rows = e_bytes.rearrange("b s k -> (b s) k")[P * lo : P * hi, :]
+            nc.sync.dma_start(out=e_raw[m][:], in_=rows.rearrange("(j p) k -> p j k", p=P))
 
         def load_d(b):
             nc.sync.dma_start(out=d_raw[b][:], in_=d[b].rearrange("(p j) k -> p j k", j=TILES))
@@ -110,18 +112,17 @@ def tile_biaffinearclogprobabilities_w4_kernel(
                 in_=vec.rearrange("(j t r) -> t j r", t=4, r=8),
             )
 
+        load_e(0)
+        load_d(0)
+        load_e(1)
+        load_d(1)
         load_words(uw_raw, u_mat_words)
         load_words(ww_raw, wh_words)
-        load_e(0)
-        load_e(1)
-        load_d(0)
-        load_e(2)
         load_bias(0, u_vec)
         load_bias(4, bh)
         load_scales(us_raw, u_mat_scales)
+        load_e(2)
         load_scales(ws_raw, wh_scales)
-        load_e(3)
-        load_d(1)
 
         def spread_scale(g, copy):
             acc = bank("spread", [P, 4, P], F32)
@@ -132,7 +133,7 @@ def tile_biaffinearclogprobabilities_w4_kernel(
 
         def scale_e(n):
             nc.vector.tensor_tensor(
-                out=e_bf[n][:], in0=e_raw[n // 2][:, n % 2, :].bitcast(FP8), in1=scale_all[:], op=ALU.mult
+                out=e_bf[n][:], in0=e_tile[n].bitcast(FP8), in1=scale_all[:], op=ALU.mult
             )
 
         def turn_e(n):
@@ -237,7 +238,7 @@ def tile_biaffinearclogprobabilities_w4_kernel(
             cols = slice(512 * g, 512 * g + 512)
             nc.vector.tensor_tensor(
                 out=e_bf[n][:, cols],
-                in0=e_raw[n // 2][:, n % 2, cols].bitcast(FP8),
+                in0=e_tile[n][:, cols].bitcast(FP8),
                 in1=scale_all[:, cols],
                 op=ALU.mult,
             )
@@ -269,7 +270,7 @@ def tile_biaffinearclogprobabilities_w4_kernel(
 
         def row_sum(b, i):
             nc.scalar.activation(
-                out=exp_out[:],
+                out=exp_out[i % 2][:],
                 in_=neg_s[TILES * b + i][:],
                 func=ACT.Exp,
                 bias=neg_max[b][:, i : i + 1],
@@ -300,65 +301,65 @@ def tile_biaffinearclogprobabilities_w4_kernel(
             )
             store(b, i)
 
-        reorder(uw, uw_raw)
-        reorder(ww, ww_raw)
         spread_scale(0, nc.scalar.copy)
         spread_scale(1, nc.scalar.copy)
         scale_e_half(0, 0)
         scale_e_half(0, 1)
-        scale_e(1)
-        turn_e(0)
         turn_d(0, 0)
         turn_d(0, 1)
+        scale_e(1)
+        turn_e(0)
+        quant_d(0)
         scale_e(2)
         turn_e(1)
-        turn_bias()
+        turn_d(1, 0)
+        reorder(uw, uw_raw)
+        reorder(us, us_raw)
         scale_e(3)
         turn_e(2)
-        quant_d(0)
-        reorder(us, us_raw)
-        scale_e(4)
+        turn_bias()
         turn_e(3)
         q_plane(0, 0)
         q_plane(0, 1)
-        reorder(ws, ws_raw)
-        quant_e(0, 0)
         q_plane(0, 2)
         q_plane(0, 3)
-        turn_e(4)
+        scale_e(4)
+        reorder(ww, ww_raw)
+        reorder(ws, ws_raw)
+        quant_e(0, 0)
         quant_e(0, 1)
-        scale_e(5)
+        turn_d(1, 1)
+        turn_e(4)
         z_plane(0, 0)
         z_plane(0, 1)
-        turn_e(5)
-        q_weave(0, 0)
-        scale_e(6)
-        turn_d(1, 0)
-        turn_d(1, 1)
         z_plane(0, 2)
         z_plane(0, 3)
-        turn_e(6)
+        scale_e(5)
+        scale_e(6)
         scale_e(7)
+        turn_e(5)
+        turn_e(6)
         turn_e(7)
-        q_weave(0, 1)
         quant_d(1)
+        q_weave(0, 0)
+        q_weave(0, 1)
+        leaky(0, 0)
+        quant_q(0, 0)
+        quant_q(0, 1)
+        quant_e(1, 0)
+        quant_e(1, 1)
         q_plane(1, 0)
         q_plane(1, 1)
         q_plane(1, 2)
         q_plane(1, 3)
-        leaky(0, 0)
-        quant_e(1, 0)
-        quant_e(1, 1)
+        leaky(0, 1)
+        quant_h(0)
         z_plane(1, 0)
         z_plane(1, 1)
-        leaky(0, 1)
-        quant_q(0, 0)
-        quant_h(0)
         z_plane(1, 2)
-        z_plane(1, 3)
         s_matmul(0, 0)
         s_matmul(0, 1)
-        quant_q(0, 1)
+        z_plane(1, 3)
         s_matmul(0, 2)
         s_matmul(0, 3)
         q_weave(1, 0)
@@ -378,11 +379,12 @@ def tile_biaffinearclogprobabilities_w4_kernel(
         s_matmul(1, 0)
         s_matmul(1, 1)
         q_weave(1, 1)
-        row_max(1, 0)
-        row_sum(1, 0)
+        row_shift(0)
         quant_q(1, 1)
         s_matmul(1, 2)
         s_matmul(1, 3)
+        row_max(1, 0)
+        row_sum(1, 0)
         row_max(1, 1)
         row_sum(1, 1)
         row_max(1, 2)
@@ -390,7 +392,6 @@ def tile_biaffinearclogprobabilities_w4_kernel(
         row_max(1, 3)
         row_sum(1, 3)
         row_log(1)
-        row_shift(0)
         finish_on_vector(0, 0)
         finish_on_vector(0, 1)
         finish_on_vector(0, 2)

@@ -64,7 +64,7 @@ def tile_biaffinearclogprobabilities_w4_kernel(
         ws = keep("ws", [P, E_PASSES, D], U8)
         bias_rows = keep("bias_rows", [P, P], BF16)
         bias = keep("bias", [P, 8], F32)
-        x_planes = [keep("x_planes%d" % b, [P, 4, S], F32) for b in range(B)]
+        x_planes = [keep("x_planes%d" % b, [P, P, 4, 4], F32) for b in range(B)]
         h_grp = [keep("h_grp%d" % b, [P, S, 4], BF16) for b in range(B)]
         h_codes = [keep("h_codes%d" % b, [P, S], U32) for b in range(B)]
         h_scl = [keep("h_scl%d" % b, [P, S], U8) for b in range(B)]
@@ -118,10 +118,10 @@ def tile_biaffinearclogprobabilities_w4_kernel(
         load_d(1)
         load_words(uw_raw, u_mat_words)
         load_words(ww_raw, wh_words)
+        load_e(2)
+        load_scales(us_raw, u_mat_scales)
         load_bias(0, u_vec)
         load_bias(4, bh)
-        load_scales(us_raw, u_mat_scales)
-        load_e(2)
         load_scales(ws_raw, wh_scales)
 
         def spread_scale(g, copy):
@@ -195,15 +195,18 @@ def tile_biaffinearclogprobabilities_w4_kernel(
                     stop=(g == E_PASSES - 1),
                 )
             nc.scalar.activation(
-                out=x_planes[b][:, t, :], in_=acc[:], func=ACT.Identity, bias=bias[:, 4 + t : 5 + t], scale=1.0
+                out=x_planes[b][:, :, t, :],
+                in_=acc[:].rearrange("p (i c) -> p c i", i=4),
+                func=ACT.Identity,
+                bias=bias[:, 4 + t : 5 + t],
+                scale=1.0,
             )
 
         def leaky(b, half):
-            cols = slice(256 * half, 256 * half + 256)
-            x = x_planes[b][:, :, cols].rearrange("p t n -> p n t")
-            nc.vector.scalar_tensor_tensor(
-                out=h_grp[b][:, cols, :], in0=x, scalar=SLOPE, in1=x, op0=ALU.mult, op1=ALU.max
-            )
+            pair = slice(2 * half, 2 * half + 2)
+            x = x_planes[b][:].rearrange("p c t i -> p (c t) i")[:, :, pair]
+            h = h_grp[b][:].rearrange("p (i c) t -> p (c t) i", i=4)[:, :, pair]
+            nc.vector.scalar_tensor_tensor(out=h, in0=x, scalar=SLOPE, in1=x, op0=ALU.mult, op1=ALU.max)
 
         def q_plane(b, t):
             acc = bank("q", [P, S], F32)
@@ -225,13 +228,6 @@ def tile_biaffinearclogprobabilities_w4_kernel(
             nc.vector.tensor_copy(
                 out=q_grp[b][:, cols, :].rearrange("p (c i) t -> p c t i", i=4),
                 in_=q_planes[b][:, :, cols].rearrange("p t (c i) -> p c t i", i=4),
-            )
-
-        def leaky4(b, quarter):
-            cols = slice(P * quarter, P * quarter + P)
-            x = x_planes[b][:, :, cols].rearrange("p t n -> p n t")
-            nc.vector.scalar_tensor_tensor(
-                out=h_grp[b][:, cols, :], in0=x, scalar=SLOPE, in1=x, op0=ALU.mult, op1=ALU.max
             )
 
         def scale_e_half(n, g):
@@ -309,16 +305,17 @@ def tile_biaffinearclogprobabilities_w4_kernel(
         turn_d(0, 1)
         scale_e(1)
         turn_e(0)
-        quant_d(0)
         scale_e(2)
         turn_e(1)
         turn_d(1, 0)
+        scale_e(3)
+        quant_d(0)
+        turn_e(2)
         reorder(uw, uw_raw)
         reorder(us, us_raw)
-        scale_e(3)
-        turn_e(2)
-        turn_bias()
         turn_e(3)
+        turn_d(1, 1)
+        turn_bias()
         q_plane(0, 0)
         q_plane(0, 1)
         q_plane(0, 2)
@@ -328,7 +325,6 @@ def tile_biaffinearclogprobabilities_w4_kernel(
         reorder(ws, ws_raw)
         quant_e(0, 0)
         quant_e(0, 1)
-        turn_d(1, 1)
         turn_e(4)
         z_plane(0, 0)
         z_plane(0, 1)
@@ -345,7 +341,6 @@ def tile_biaffinearclogprobabilities_w4_kernel(
         q_weave(0, 1)
         leaky(0, 0)
         quant_q(0, 0)
-        quant_q(0, 1)
         quant_e(1, 0)
         quant_e(1, 1)
         q_plane(1, 0)
@@ -353,6 +348,7 @@ def tile_biaffinearclogprobabilities_w4_kernel(
         q_plane(1, 2)
         q_plane(1, 3)
         leaky(0, 1)
+        quant_q(0, 1)
         quant_h(0)
         z_plane(1, 0)
         z_plane(1, 1)

@@ -20,8 +20,14 @@ ALU = mybir.AluOpType
 ACT = mybir.ActivationFunctionType
 
 P = 128
+SLOTS = 4
+K_PASS = P * SLOTS
 TILES = S // P
-E_PASSES = E // 512
+E_PASSES = E // K_PASS
+HALF = S // 2
+BLOCKS = 16
+PSUM_BANKS = 8
+E_LOADS = ((0, 1), (1, TILES), (TILES, B * TILES))
 
 
 def tile_biaffinearclogprobabilities_w4_kernel(
@@ -30,30 +36,35 @@ def tile_biaffinearclogprobabilities_w4_kernel(
     nc = tc.nc
     with ExitStack() as ctx:
         sb = ctx.enter_context(tc.tile_pool(name="sb", bufs=1))
-        ps = ctx.enter_context(tc.psum_pool(name="ps", bufs=8))
+        ps = ctx.enter_context(tc.psum_pool(name="ps", bufs=PSUM_BANKS))
         ctx.enter_context(tc.manual_schedule())
 
         def keep(name, shape, dtype):
             return sb.tile(shape, dtype, name=name, tag=name, align_bytes=64)
+
+        def per_sentence(name, shape, dtype):
+            return [keep("%s%d" % (name, b), shape, dtype) for b in range(B)]
+
+        def per_tile(name, shape, dtype):
+            return [keep("%s%d" % (name, n), shape, dtype) for n in range(B * TILES)]
 
         def bank(name, shape, dtype):
             return ps.tile(shape, dtype, name=name, tag="bank")
 
         ident32 = keep("ident32", [P, P], F32)
         ident16 = keep("ident16", [P, P], BF16)
-        scale_col = keep("scale_col", [P, E_PASSES, 4], F32)
+        scale_col = keep("scale_col", [P, E_PASSES, 2 * SLOTS], F32)
         scale_all = keep("scale_all", [P, E], F32)
-        e_loads = ((0, 1), (1, 4), (4, 8))
-        e_raw = [keep("e_raw%d" % lo, [P, hi - lo, E], U8) for lo, hi in e_loads]
-        e_tile = [e_raw[m][:, n - lo, :] for m, (lo, hi) in enumerate(e_loads) for n in range(lo, hi)]
-        e_bf = [keep("e_bf%d" % n, [P, E], BF16) for n in range(B * TILES)]
-        e_grp = [keep("e_grp%d" % b, [P, E_PASSES, S, 2], F32) for b in range(B)]
-        e_codes = [keep("e_codes%d" % b, [P, E_PASSES, S], U32) for b in range(B)]
-        e_scl = [keep("e_scl%d" % b, [P, E_PASSES, S], U8) for b in range(B)]
-        d_raw = [keep("d_raw%d" % b, [P, TILES, D], BF16) for b in range(B)]
-        d_grp = [keep("d_grp%d" % b, [P, S, 2], F32) for b in range(B)]
-        d_codes = [keep("d_codes%d" % b, [P, S], U32) for b in range(B)]
-        d_scl = [keep("d_scl%d" % b, [P, S], U8) for b in range(B)]
+        e_raw = [keep("e_raw%d" % lo, [P, hi - lo, E], U8) for lo, hi in E_LOADS]
+        e_tile = [e_raw[m][:, n - lo, :] for m, (lo, hi) in enumerate(E_LOADS) for n in range(lo, hi)]
+        e_bf = per_tile("e_bf", [P, E], BF16)
+        e_grp = per_sentence("e_grp", [P, E_PASSES, S, 2], F32)
+        e_codes = per_sentence("e_codes", [P, E_PASSES, S], U32)
+        e_scl = per_sentence("e_scl", [P, E_PASSES, S], U8)
+        d_raw = per_sentence("d_raw", [P, TILES, D], BF16)
+        d_grp = per_sentence("d_grp", [P, S, 2], F32)
+        d_codes = per_sentence("d_codes", [P, S], U32)
+        d_scl = per_sentence("d_scl", [P, S], U8)
         uw_raw = keep("uw_raw", [P, 1, 2 * D], U8)
         ww_raw = keep("ww_raw", [P, E_PASSES, 2 * D], U8)
         us_raw = keep("us_raw", [P, 1, D], U8)
@@ -63,23 +74,23 @@ def tile_biaffinearclogprobabilities_w4_kernel(
         us = keep("us", [P, 1, D], U8)
         ws = keep("ws", [P, E_PASSES, D], U8)
         bias_rows = keep("bias_rows", [P, P], BF16)
-        bias = keep("bias", [P, 8], F32)
-        x_planes = [keep("x_planes%d" % b, [P, P, 4, 4], F32) for b in range(B)]
-        h_grp = [keep("h_grp%d" % b, [P, S, 4], BF16) for b in range(B)]
-        h_codes = [keep("h_codes%d" % b, [P, S], U32) for b in range(B)]
-        h_scl = [keep("h_scl%d" % b, [P, S], U8) for b in range(B)]
-        q_grp = [keep("q_grp%d" % b, [P, S, 4], BF16) for b in range(B)]
-        q_codes = [keep("q_codes%d" % b, [P, S], U32) for b in range(B)]
-        q_scl = [keep("q_scl%d" % b, [P, S], U8) for b in range(B)]
-        neg_s = [keep("neg_s%d" % n, [P, S], F32) for n in range(B * TILES)]
-        res = [keep("res%d" % n, [P, S], F32) for n in range(B * TILES)]
+        bias = keep("bias", [P, 2 * SLOTS], F32)
+        z_lines = per_sentence("z_lines", [P, P, SLOTS, TILES], F32)
+        h_grp = per_sentence("h_grp", [P, S, SLOTS], BF16)
+        h_codes = per_sentence("h_codes", [P, S], U32)
+        h_scl = per_sentence("h_scl", [P, S], U8)
+        q_grp = per_sentence("q_grp", [P, S, SLOTS], BF16)
+        q_codes = per_sentence("q_codes", [P, S], U32)
+        q_scl = per_sentence("q_scl", [P, S], U8)
+        neg_s = per_tile("neg_s", [P, S], F32)
+        res = per_tile("res", [P, S], F32)
         exp_out = [keep("exp_out%d" % n, [P, S], BF16) for n in range(2)]
-        neg_max = [keep("neg_max%d" % b, [P, TILES], F32) for b in range(B)]
-        sums = [keep("sums%d" % b, [P, TILES], F32) for b in range(B)]
-        q_planes = [keep("q_planes%d" % b, [P, 4, S], BF16) for b in range(B)]
-        logs = [keep("logs%d" % b, [P, TILES], F32) for b in range(B)]
-        shift = [keep("shift%d" % b, [P, TILES], F32) for b in range(B)]
-        banks = {}
+        neg_max = per_sentence("neg_max", [P, TILES], F32)
+        sums = per_sentence("sums", [P, TILES], F32)
+        q_planes = per_sentence("q_planes", [P, SLOTS, S], BF16)
+        logs = per_sentence("logs", [P, TILES], F32)
+        shift = keep("shift", [P, TILES], F32)
+        scores = {}
 
         make_identity(nc, ident32[:])
         nc.vector.memset(bias_rows[:], 0.0)
@@ -88,14 +99,13 @@ def tile_biaffinearclogprobabilities_w4_kernel(
         nc.scalar.activation(out=ident16[:], in_=ident32[:], func=ACT.Copy)
 
         def load_e(m):
-            lo, hi = e_loads[m]
+            lo, hi = E_LOADS[m]
             rows = e_bytes.rearrange("b s k -> (b s) k")[P * lo : P * hi, :]
             nc.sync.dma_start(out=e_raw[m][:], in_=rows.rearrange("(j p) k -> p j k", p=P))
 
         def load_d(b):
-            nc.sync.dma_start(out=d_raw[b][:], in_=d[b].rearrange("(p j) k -> p j k", j=TILES))
+            nc.sync.dma_start(out=d_raw[b][:], in_=d[b].rearrange("(p i) k -> p i k", i=TILES))
 
-        nc.sync.dma_start(out=scale_col[:], in_=e_scale.rearrange("a o (g p c) -> p (a o g) c", g=E_PASSES, c=4))
         def load_words(raw, src):
             nc.sync.dma_start(out=raw[:].bitcast(I32), in_=src.bitcast(I32).rearrange("g p w -> p g w"))
 
@@ -108,10 +118,14 @@ def tile_biaffinearclogprobabilities_w4_kernel(
 
         def load_bias(row, vec):
             nc.sync.dma_start(
-                out=bias_rows[row : row + 4, :].rearrange("t (j r) -> t j r", r=8),
-                in_=vec.rearrange("(j t r) -> t j r", t=4, r=8),
+                out=bias_rows[row : row + SLOTS, :].rearrange("t (j r) -> t j r", j=BLOCKS),
+                in_=vec.rearrange("(j t r) -> t j r", j=BLOCKS, t=SLOTS),
             )
 
+        nc.sync.dma_start(
+            out=scale_col[:, :, 0:SLOTS],
+            in_=e_scale.rearrange("a o (g p t) -> p (a o g) t", g=E_PASSES, t=SLOTS),
+        )
         load_e(0)
         load_d(0)
         load_e(1)
@@ -121,19 +135,19 @@ def tile_biaffinearclogprobabilities_w4_kernel(
         load_e(2)
         load_scales(us_raw, u_mat_scales)
         load_bias(0, u_vec)
-        load_bias(4, bh)
+        load_bias(SLOTS, bh)
         load_scales(ws_raw, wh_scales)
 
-        def spread_scale(g, copy):
-            acc = bank("spread", [P, 4, P], F32)
-            for c in range(4):
-                nc.tensor.transpose(acc[:, c, :], scale_col[:, g, c : c + 1].to_broadcast([P, P]), ident32[:])
-            dst = scale_all[:, 512 * g : 512 * g + 512].rearrange("p (n c) -> p n c", c=4)
-            copy(out=dst, in_=acc[:].rearrange("p c n -> p n c"))
+        def spread_scale(g):
+            acc = bank("spread", [P, SLOTS, P], F32)
+            for t in range(SLOTS):
+                nc.tensor.transpose(acc[:, t, :], scale_col[:, g, t : t + 1].to_broadcast([P, P]), ident32[:])
+            dst = scale_all[:, K_PASS * g : K_PASS * (g + 1)].rearrange("p (m t) -> p m t", t=SLOTS)
+            nc.scalar.copy(out=dst, in_=acc[:].rearrange("p t m -> p m t"))
 
-        def scale_e(n):
+        def scale_e(n, cols=slice(0, E)):
             nc.vector.tensor_tensor(
-                out=e_bf[n][:], in0=e_tile[n].bitcast(FP8), in1=scale_all[:], op=ALU.mult
+                out=e_bf[n][:, cols], in0=e_tile[n][:, cols].bitcast(FP8), in1=scale_all[:, cols], op=ALU.mult
             )
 
         def turn_e(n):
@@ -142,44 +156,45 @@ def tile_biaffinearclogprobabilities_w4_kernel(
             words = e_bf[n][:].bitcast(F32)
             for g in range(E_PASSES):
                 for u in range(2):
-                    nc.tensor.transpose(acc[:, g, u, :], words[:, 256 * g + u : 256 * g + 256 : 2], ident32[:])
-            nc.scalar.copy(out=e_grp[b][:, :, P * j : P * j + P, :], in_=acc[:].rearrange("p g u r -> p g r u"))
+                    nc.tensor.transpose(acc[:, g, u, :], words[:, 2 * P * g + u : 2 * P * (g + 1) : 2], ident32[:])
+            nc.scalar.copy(out=e_grp[b][:, :, P * j : P * (j + 1), :], in_=acc[:].rearrange("p g u r -> p g r u"))
 
         def turn_d(b, half):
             acc = bank("turn_d", [P, 2, 2, P], F32)
-            for jj in range(2):
-                words = d_raw[b][:, 2 * half + jj, :].bitcast(F32)
+            for i in range(2):
+                words = d_raw[b][:, 2 * half + i, :].bitcast(F32)
                 for u in range(2):
-                    nc.tensor.transpose(acc[:, jj, u, :], words[:, u:256:2], ident32[:])
-            dst = d_grp[b][:, 256 * half : 256 * half + 256, :].rearrange("p (j r) u -> p j r u", j=2)
-            nc.scalar.copy(out=dst, in_=acc[:].rearrange("p j u r -> p j r u"))
+                    nc.tensor.transpose(acc[:, i, u, :], words[:, u : 2 * P : 2], ident32[:])
+            dst = d_grp[b][:, HALF * half : HALF * (half + 1), :].rearrange("p (i r) u -> p i r u", i=2)
+            nc.scalar.copy(out=dst, in_=acc[:].rearrange("p i u r -> p i r u"))
 
         def turn_bias():
             acc = bank("turn_bias", [P, P], BF16)
             nc.tensor.transpose(acc[:], bias_rows[:], ident16[:])
-            nc.scalar.copy(out=bias[:], in_=acc[:, 0:8])
+            nc.scalar.copy(out=bias[:], in_=acc[:, 0 : 2 * SLOTS])
 
         def reorder(dst, src):
             nc.vector.tensor_copy(
-                out=dst[:].bitcast(I32).rearrange("p g (t j w) -> p g t j w", t=4, j=16),
-                in_=src[:].bitcast(I32).rearrange("p g (j t w) -> p g t j w", t=4, j=16),
+                out=dst[:].bitcast(I32).rearrange("p g (t j w) -> p g t j w", t=SLOTS, j=BLOCKS),
+                in_=src[:].bitcast(I32).rearrange("p g (j t w) -> p g t j w", t=SLOTS, j=BLOCKS),
             )
 
         def quantize(codes, scales, values):
             nc.vector.quantize_mx(out=codes.bitcast(FP8X4), scales=scales, in_=values)
 
-        def quant_e(b, g):
-            values = e_grp[b][:, g, :, :].rearrange("p r u -> p (r u)").bitcast(BF16)
-            quantize(e_codes[b][:, g, :], e_scl[b][:, g, :], values)
+        def quant_e(b):
+            for g in range(E_PASSES):
+                values = e_grp[b][:, g, :, :].rearrange("p n u -> p (n u)").bitcast(BF16)
+                quantize(e_codes[b][:, g, :], e_scl[b][:, g, :], values)
 
         def quant_d(b):
-            quantize(d_codes[b][:], d_scl[b][:], d_grp[b][:].rearrange("p r u -> p (r u)").bitcast(BF16))
+            quantize(d_codes[b][:], d_scl[b][:], d_grp[b][:].rearrange("p n u -> p (n u)").bitcast(BF16))
 
         def quant_h(b):
             quantize(h_codes[b][:], h_scl[b][:], h_grp[b][:].rearrange("p n t -> p (n t)"))
 
         def quant_q(b, half):
-            cols = slice(256 * half, 256 * half + 256)
+            cols = slice(HALF * half, HALF * (half + 1))
             quantize(q_codes[b][:, cols], q_scl[b][:, cols], q_grp[b][:, cols, :].rearrange("p n t -> p (n t)"))
 
         def z_plane(b, t):
@@ -187,33 +202,33 @@ def tile_biaffinearclogprobabilities_w4_kernel(
             for g in range(E_PASSES):
                 nc.tensor.matmul_mx(
                     out=acc[:],
-                    lhsT=ww[:, g, 256 * t : 256 * t + 256].bitcast(FP4X4),
-                    lhsT_scale=ws[:, g, P * t : P * t + P],
+                    lhsT=ww[:, g, 2 * P * t : 2 * P * (t + 1)].bitcast(FP4X4),
+                    lhsT_scale=ws[:, g, P * t : P * (t + 1)],
                     rhs=e_codes[b][:, g, :].bitcast(FP8X4),
                     rhs_scale=e_scl[b][:, g, :],
                     start=(g == 0),
                     stop=(g == E_PASSES - 1),
                 )
             nc.scalar.activation(
-                out=x_planes[b][:, :, t, :],
-                in_=acc[:].rearrange("p (i c) -> p c i", i=4),
+                out=z_lines[b][:, :, t, :],
+                in_=acc[:].rearrange("p (i c) -> p c i", i=TILES),
                 func=ACT.Identity,
-                bias=bias[:, 4 + t : 5 + t],
+                bias=bias[:, SLOTS + t : SLOTS + t + 1],
                 scale=1.0,
             )
 
         def leaky(b, half):
             pair = slice(2 * half, 2 * half + 2)
-            x = x_planes[b][:].rearrange("p c t i -> p (c t) i")[:, :, pair]
-            h = h_grp[b][:].rearrange("p (i c) t -> p (c t) i", i=4)[:, :, pair]
-            nc.vector.scalar_tensor_tensor(out=h, in0=x, scalar=SLOPE, in1=x, op0=ALU.mult, op1=ALU.max)
+            z = z_lines[b][:].rearrange("p c t i -> p (c t) i")[:, :, pair]
+            h = h_grp[b][:].rearrange("p (i c) t -> p (c t) i", i=TILES)[:, :, pair]
+            nc.vector.scalar_tensor_tensor(out=h, in0=z, scalar=SLOPE, in1=z, op0=ALU.mult, op1=ALU.max)
 
         def q_plane(b, t):
             acc = bank("q", [P, S], F32)
             nc.tensor.matmul_mx(
                 out=acc[:],
-                lhsT=uw[:, 0, 256 * t : 256 * t + 256].bitcast(FP4X4),
-                lhsT_scale=us[:, 0, P * t : P * t + P],
+                lhsT=uw[:, 0, 2 * P * t : 2 * P * (t + 1)].bitcast(FP4X4),
+                lhsT_scale=us[:, 0, P * t : P * (t + 1)],
                 rhs=d_codes[b][:].bitcast(FP8X4),
                 rhs_scale=d_scl[b][:],
                 start=True,
@@ -224,25 +239,16 @@ def tile_biaffinearclogprobabilities_w4_kernel(
             )
 
         def q_weave(b, half):
-            cols = slice(256 * half, 256 * half + 256)
+            cols = slice(HALF * half, HALF * (half + 1))
             nc.vector.tensor_copy(
-                out=q_grp[b][:, cols, :].rearrange("p (c i) t -> p c t i", i=4),
-                in_=q_planes[b][:, :, cols].rearrange("p t (c i) -> p c t i", i=4),
-            )
-
-        def scale_e_half(n, g):
-            cols = slice(512 * g, 512 * g + 512)
-            nc.vector.tensor_tensor(
-                out=e_bf[n][:, cols],
-                in0=e_tile[n][:, cols].bitcast(FP8),
-                in1=scale_all[:, cols],
-                op=ALU.mult,
+                out=q_grp[b][:, cols, :].rearrange("p (c w) t -> p c t w", w=4),
+                in_=q_planes[b][:, :, cols].rearrange("p t (c w) -> p c t w", w=4),
             )
 
         def s_matmul(b, i):
             acc = bank("s", [P, S], F32)
-            banks[("s", b, i)] = acc
-            cols = slice(P * i, P * i + P)
+            scores[(b, i)] = acc
+            cols = slice(P * i, P * (i + 1))
             nc.tensor.matmul_mx(
                 out=acc[:],
                 lhsT=q_codes[b][:, cols].bitcast(FP8X4),
@@ -253,21 +259,20 @@ def tile_biaffinearclogprobabilities_w4_kernel(
                 stop=True,
             )
 
-        def row_max(b, i):
+        def row_stats(b, i):
+            n = TILES * b + i
             nc.vector.tensor_scalar(
-                out=neg_s[TILES * b + i][:],
-                in0=banks[("s", b, i)][:],
+                out=neg_s[n][:],
+                in0=scores[(b, i)][:],
                 scalar1=-1.0 / math.sqrt(D),
                 scalar2=None,
                 op0=ALU.mult,
                 op1=ALU.min,
                 accum_out=neg_max[b][:, i : i + 1],
             )
-
-        def row_sum(b, i):
             nc.scalar.activation(
                 out=exp_out[i % 2][:],
-                in_=neg_s[TILES * b + i][:],
+                in_=neg_s[n][:],
                 func=ACT.Exp,
                 bias=neg_max[b][:, i : i + 1],
                 scale=-1.0,
@@ -277,30 +282,40 @@ def tile_biaffinearclogprobabilities_w4_kernel(
         def row_log(b):
             nc.scalar.activation(out=logs[b][:], in_=sums[b][:], func=ACT.Ln)
 
-        def row_shift(b):
-            nc.vector.tensor_tensor(out=shift[b][:], in0=neg_max[b][:], in1=logs[b][:], op=ALU.subtract)
-
         def store(b, i):
-            nc.sync.dma_start(out=out[b].rearrange("(p j) n -> j p n", j=TILES)[i], in_=res[TILES * b + i][:])
+            nc.sync.dma_start(out=out[b].rearrange("(p i) n -> i p n", i=TILES)[i], in_=res[TILES * b + i][:])
 
-        def finish_on_scalar(b, i):
-            n = TILES * b + i
-            nc.scalar.activation(
-                out=res[n][:], in_=neg_s[n][:], func=ACT.Identity, bias=shift[b][:, i : i + 1], scale=-1.0
+        def finish_first(i, engine):
+            engine.tensor_scalar(
+                out=res[i][:], in0=neg_s[i][:], scalar1=-1.0, scalar2=shift[:, i : i + 1], op0=ALU.mult, op1=ALU.add
             )
-            store(b, i)
+            store(0, i)
 
-        def finish_on_vector(b, i):
-            n = TILES * b + i
+        def centre_last(i):
             nc.vector.tensor_scalar(
-                out=res[n][:], in0=neg_s[n][:], scalar1=-1.0, scalar2=shift[b][:, i : i + 1], op0=ALU.mult, op1=ALU.add
+                out=res[TILES + i][:],
+                in0=neg_s[TILES + i][:],
+                scalar1=neg_max[1][:, i : i + 1],
+                scalar2=-1.0,
+                op0=ALU.subtract,
+                op1=ALU.mult,
             )
-            store(b, i)
 
-        spread_scale(0, nc.scalar.copy)
-        spread_scale(1, nc.scalar.copy)
-        scale_e_half(0, 0)
-        scale_e_half(0, 1)
+        def finish_last(i):
+            nc.vector.tensor_scalar(
+                out=res[TILES + i][:],
+                in0=res[TILES + i][:],
+                scalar1=logs[1][:, i : i + 1],
+                scalar2=None,
+                op0=ALU.subtract,
+            )
+            store(1, i)
+
+
+        for g in range(E_PASSES):
+            spread_scale(g)
+        for g in range(E_PASSES):
+            scale_e(0, slice(K_PASS * g, K_PASS * (g + 1)))
         turn_d(0, 0)
         turn_d(0, 1)
         scale_e(1)
@@ -315,58 +330,45 @@ def tile_biaffinearclogprobabilities_w4_kernel(
         reorder(us, us_raw)
         turn_e(3)
         turn_d(1, 1)
+
         turn_bias()
-        q_plane(0, 0)
-        q_plane(0, 1)
-        q_plane(0, 2)
-        q_plane(0, 3)
-        scale_e(4)
+        for t in range(SLOTS):
+            q_plane(0, t)
+        scale_e(TILES)
         reorder(ww, ww_raw)
         reorder(ws, ws_raw)
-        quant_e(0, 0)
-        quant_e(0, 1)
-        turn_e(4)
-        z_plane(0, 0)
-        z_plane(0, 1)
-        z_plane(0, 2)
-        z_plane(0, 3)
-        scale_e(5)
-        scale_e(6)
-        scale_e(7)
-        turn_e(5)
-        turn_e(6)
-        turn_e(7)
+        quant_e(0)
+        turn_e(TILES)
+        for t in range(SLOTS):
+            z_plane(0, t)
+        for n in range(TILES + 1, B * TILES):
+            scale_e(n)
+        for n in range(TILES + 1, B * TILES):
+            turn_e(n)
+
         quant_d(1)
         q_weave(0, 0)
         q_weave(0, 1)
         leaky(0, 0)
         quant_q(0, 0)
-        quant_e(1, 0)
-        quant_e(1, 1)
-        q_plane(1, 0)
-        q_plane(1, 1)
-        q_plane(1, 2)
-        q_plane(1, 3)
+        quant_e(1)
+        for t in range(SLOTS):
+            q_plane(1, t)
         leaky(0, 1)
         quant_q(0, 1)
         quant_h(0)
-        z_plane(1, 0)
-        z_plane(1, 1)
-        z_plane(1, 2)
+
+        for t in range(SLOTS - 1):
+            z_plane(1, t)
         s_matmul(0, 0)
         s_matmul(0, 1)
-        z_plane(1, 3)
+        z_plane(1, SLOTS - 1)
         s_matmul(0, 2)
         s_matmul(0, 3)
         q_weave(1, 0)
-        row_max(0, 0)
-        row_sum(0, 0)
-        row_max(0, 1)
-        row_sum(0, 1)
-        row_max(0, 2)
-        row_sum(0, 2)
-        row_max(0, 3)
-        row_sum(0, 3)
+        for i in range(TILES):
+            row_stats(0, i)
+
         row_log(0)
         leaky(1, 0)
         leaky(1, 1)
@@ -375,25 +377,20 @@ def tile_biaffinearclogprobabilities_w4_kernel(
         s_matmul(1, 0)
         s_matmul(1, 1)
         q_weave(1, 1)
-        row_shift(0)
         quant_q(1, 1)
         s_matmul(1, 2)
         s_matmul(1, 3)
-        row_max(1, 0)
-        row_sum(1, 0)
-        row_max(1, 1)
-        row_sum(1, 1)
-        row_max(1, 2)
-        row_sum(1, 2)
-        row_max(1, 3)
-        row_sum(1, 3)
+
+        nc.vector.tensor_tensor(out=shift[:], in0=neg_max[0][:], in1=logs[0][:], op=ALU.subtract)
+        for i in range(TILES // 2):
+            finish_first(i, nc.gpsimd)
+        for i in range(TILES):
+            row_stats(1, i)
+
         row_log(1)
-        finish_on_vector(0, 0)
-        finish_on_vector(0, 1)
-        finish_on_vector(0, 2)
-        finish_on_vector(0, 3)
-        row_shift(1)
-        finish_on_vector(1, 0)
-        finish_on_vector(1, 1)
-        finish_on_scalar(1, 3)
-        finish_on_vector(1, 2)
+        for i in range(TILES // 2, TILES):
+            finish_first(i, nc.vector)
+        for i in range(TILES):
+            centre_last(i)
+        for i in range(TILES):
+            finish_last(i)

import math
from contextlib import ExitStack

import concourse.mybir as mybir
from concourse.masks import make_identity

B, S, E, D = 2, 512, 1024, 512
SLOPE = 0.1
FLOPS = 2 * B * S * (D * D + E * D + S * D)

F32 = mybir.dt.float32
BF16 = mybir.dt.bfloat16
I32 = mybir.dt.int32
U32 = mybir.dt.uint32
U8 = mybir.dt.uint8
FP8 = mybir.dt.float8_e4m3fn
FP8X4 = mybir.dt.float8_e4m3fn_x4
FP4X4 = mybir.dt.float4_e2m1fn_x4
ALU = mybir.AluOpType
ACT = mybir.ActivationFunctionType

P = 128
SLOTS = 4
K_PASS = P * SLOTS
TILES = S // P
E_PASSES = E // K_PASS
HALF = S // 2
BLOCKS = 16
PSUM_BANKS = 8
E_LOADS = ((0, 1), (1, TILES), (TILES, B * TILES))


def tile_biaffinearclogprobabilities_w4_kernel(
    tc, d, e_bytes, e_scale, u_mat_words, u_mat_scales, u_vec, wh_words, wh_scales, bh, out
):
    nc = tc.nc
    with ExitStack() as ctx:
        sb = ctx.enter_context(tc.tile_pool(name="sb", bufs=1))
        ps = ctx.enter_context(tc.psum_pool(name="ps", bufs=PSUM_BANKS))
        ctx.enter_context(tc.manual_schedule())

        def keep(name, shape, dtype):
            return sb.tile(shape, dtype, name=name, tag=name, align_bytes=64)

        def per_sentence(name, shape, dtype):
            return [keep("%s%d" % (name, b), shape, dtype) for b in range(B)]

        def per_tile(name, shape, dtype):
            return [keep("%s%d" % (name, n), shape, dtype) for n in range(B * TILES)]

        def bank(name, shape, dtype):
            return ps.tile(shape, dtype, name=name, tag="bank")

        ident32 = keep("ident32", [P, P], F32)
        ident16 = keep("ident16", [P, P], BF16)
        scale_col = keep("scale_col", [P, E_PASSES, 2 * SLOTS], F32)
        scale_all = keep("scale_all", [P, E], F32)
        e_raw = [keep("e_raw%d" % lo, [P, hi - lo, E], U8) for lo, hi in E_LOADS]
        e_tile = [e_raw[m][:, n - lo, :] for m, (lo, hi) in enumerate(E_LOADS) for n in range(lo, hi)]
        e_bf = per_tile("e_bf", [P, E], BF16)
        e_grp = per_sentence("e_grp", [P, E_PASSES, S, 2], F32)
        e_codes = per_sentence("e_codes", [P, E_PASSES, S], U32)
        e_scl = per_sentence("e_scl", [P, E_PASSES, S], U8)
        d_raw = per_sentence("d_raw", [P, TILES, D], BF16)
        d_grp = per_sentence("d_grp", [P, S, 2], F32)
        d_codes = per_sentence("d_codes", [P, S], U32)
        d_scl = per_sentence("d_scl", [P, S], U8)
        uw_raw = keep("uw_raw", [P, 1, 2 * D], U8)
        ww_raw = keep("ww_raw", [P, E_PASSES, 2 * D], U8)
        us_raw = keep("us_raw", [P, 1, D], U8)
        ws_raw = keep("ws_raw", [P, E_PASSES, D], U8)
        uw = keep("uw", [P, 1, 2 * D], U8)
        ww = keep("ww", [P, E_PASSES, 2 * D], U8)
        us = keep("us", [P, 1, D], U8)
        ws = keep("ws", [P, E_PASSES, D], U8)
        bias_rows = keep("bias_rows", [P, P], BF16)
        bias = keep("bias", [P, 2 * SLOTS], F32)
        z_lines = per_sentence("z_lines", [P, P, SLOTS, TILES], F32)
        h_grp = per_sentence("h_grp", [P, S, SLOTS], BF16)
        h_codes = per_sentence("h_codes", [P, S], U32)
        h_scl = per_sentence("h_scl", [P, S], U8)
        q_grp = per_sentence("q_grp", [P, S, SLOTS], BF16)
        q_codes = per_sentence("q_codes", [P, S], U32)
        q_scl = per_sentence("q_scl", [P, S], U8)
        neg_s = per_tile("neg_s", [P, S], F32)
        res = per_tile("res", [P, S], F32)
        exp_out = [keep("exp_out%d" % n, [P, S], BF16) for n in range(2)]
        neg_max = per_sentence("neg_max", [P, TILES], F32)
        sums = per_sentence("sums", [P, TILES], F32)
        q_planes = per_sentence("q_planes", [P, SLOTS, S], BF16)
        logs = per_sentence("logs", [P, TILES], F32)
        shift = keep("shift", [P, TILES], F32)
        scores = {}

        make_identity(nc, ident32[:])
        nc.vector.memset(bias_rows[:], 0.0)
        nc.vector.memset(us_raw[:].bitcast(I32), 0)
        nc.vector.memset(ws_raw[:].bitcast(I32), 0)
        nc.scalar.activation(out=ident16[:], in_=ident32[:], func=ACT.Copy)

        def load_e(m):
            lo, hi = E_LOADS[m]
            rows = e_bytes.rearrange("b s k -> (b s) k")[P * lo : P * hi, :]
            nc.sync.dma_start(out=e_raw[m][:], in_=rows.rearrange("(j p) k -> p j k", p=P))

        def load_d(b):
            nc.sync.dma_start(out=d_raw[b][:], in_=d[b].rearrange("(p i) k -> p i k", i=TILES))

        def load_words(raw, src):
            nc.sync.dma_start(out=raw[:].bitcast(I32), in_=src.bitcast(I32).rearrange("g p w -> p g w"))

        def load_scales(raw, src):
            for quad in range(4):
                nc.sync.dma_start(
                    out=raw[32 * quad : 32 * quad + 4, :, :].bitcast(I32),
                    in_=src.bitcast(I32)[:, 4 * quad : 4 * quad + 4, :].rearrange("g r w -> r g w"),
                )

        def load_bias(row, vec):
            nc.sync.dma_start(
                out=bias_rows[row : row + SLOTS, :].rearrange("t (j r) -> t j r", j=BLOCKS),
                in_=vec.rearrange("(j t r) -> t j r", j=BLOCKS, t=SLOTS),
            )

        nc.sync.dma_start(
            out=scale_col[:, :, 0:SLOTS],
            in_=e_scale.rearrange("a o (g p t) -> p (a o g) t", g=E_PASSES, t=SLOTS),
        )
        load_e(0)
        load_d(0)
        load_e(1)
        load_d(1)
        load_words(uw_raw, u_mat_words)
        load_words(ww_raw, wh_words)
        load_e(2)
        load_scales(us_raw, u_mat_scales)
        load_bias(0, u_vec)
        load_bias(SLOTS, bh)
        load_scales(ws_raw, wh_scales)

        def spread_scale(g):
            acc = bank("spread", [P, SLOTS, P], F32)
            for t in range(SLOTS):
                nc.tensor.transpose(acc[:, t, :], scale_col[:, g, t : t + 1].to_broadcast([P, P]), ident32[:])
            dst = scale_all[:, K_PASS * g : K_PASS * (g + 1)].rearrange("p (m t) -> p m t", t=SLOTS)
            nc.scalar.copy(out=dst, in_=acc[:].rearrange("p t m -> p m t"))

        def scale_e(n, cols=slice(0, E)):
            nc.vector.tensor_tensor(
                out=e_bf[n][:, cols], in0=e_tile[n][:, cols].bitcast(FP8), in1=scale_all[:, cols], op=ALU.mult
            )

        def turn_e(n):
            b, j = divmod(n, TILES)
            acc = bank("turn_e", [P, E_PASSES, 2, P], F32)
            words = e_bf[n][:].bitcast(F32)
            for g in range(E_PASSES):
                for u in range(2):
                    nc.tensor.transpose(acc[:, g, u, :], words[:, 2 * P * g + u : 2 * P * (g + 1) : 2], ident32[:])
            nc.scalar.copy(out=e_grp[b][:, :, P * j : P * (j + 1), :], in_=acc[:].rearrange("p g u r -> p g r u"))

        def turn_d(b, half):
            acc = bank("turn_d", [P, 2, 2, P], F32)
            for i in range(2):
                words = d_raw[b][:, 2 * half + i, :].bitcast(F32)
                for u in range(2):
                    nc.tensor.transpose(acc[:, i, u, :], words[:, u : 2 * P : 2], ident32[:])
            dst = d_grp[b][:, HALF * half : HALF * (half + 1), :].rearrange("p (i r) u -> p i r u", i=2)
            nc.scalar.copy(out=dst, in_=acc[:].rearrange("p i u r -> p i r u"))

        def turn_bias():
            acc = bank("turn_bias", [P, P], BF16)
            nc.tensor.transpose(acc[:], bias_rows[:], ident16[:])
            nc.scalar.copy(out=bias[:], in_=acc[:, 0 : 2 * SLOTS])

        def reorder(dst, src):
            nc.vector.tensor_copy(
                out=dst[:].bitcast(I32).rearrange("p g (t j w) -> p g t j w", t=SLOTS, j=BLOCKS),
                in_=src[:].bitcast(I32).rearrange("p g (j t w) -> p g t j w", t=SLOTS, j=BLOCKS),
            )

        def quantize(codes, scales, values):
            nc.vector.quantize_mx(out=codes.bitcast(FP8X4), scales=scales, in_=values)

        def quant_e(b):
            for g in range(E_PASSES):
                values = e_grp[b][:, g, :, :].rearrange("p n u -> p (n u)").bitcast(BF16)
                quantize(e_codes[b][:, g, :], e_scl[b][:, g, :], values)

        def quant_d(b):
            quantize(d_codes[b][:], d_scl[b][:], d_grp[b][:].rearrange("p n u -> p (n u)").bitcast(BF16))

        def quant_h(b):
            quantize(h_codes[b][:], h_scl[b][:], h_grp[b][:].rearrange("p n t -> p (n t)"))

        def quant_q(b, half):
            cols = slice(HALF * half, HALF * (half + 1))
            quantize(q_codes[b][:, cols], q_scl[b][:, cols], q_grp[b][:, cols, :].rearrange("p n t -> p (n t)"))

        def z_plane(b, t):
            acc = bank("z", [P, S], F32)
            for g in range(E_PASSES):
                nc.tensor.matmul_mx(
                    out=acc[:],
                    lhsT=ww[:, g, 2 * P * t : 2 * P * (t + 1)].bitcast(FP4X4),
                    lhsT_scale=ws[:, g, P * t : P * (t + 1)],
                    rhs=e_codes[b][:, g, :].bitcast(FP8X4),
                    rhs_scale=e_scl[b][:, g, :],
                    start=(g == 0),
                    stop=(g == E_PASSES - 1),
                )
            nc.scalar.activation(
                out=z_lines[b][:, :, t, :],
                in_=acc[:].rearrange("p (i c) -> p c i", i=TILES),
                func=ACT.Identity,
                bias=bias[:, SLOTS + t : SLOTS + t + 1],
                scale=1.0,
            )

        def leaky(b, half):
            pair = slice(2 * half, 2 * half + 2)
            z = z_lines[b][:].rearrange("p c t i -> p (c t) i")[:, :, pair]
            h = h_grp[b][:].rearrange("p (i c) t -> p (c t) i", i=TILES)[:, :, pair]
            nc.vector.scalar_tensor_tensor(out=h, in0=z, scalar=SLOPE, in1=z, op0=ALU.mult, op1=ALU.max)

        def q_plane(b, t):
            acc = bank("q", [P, S], F32)
            nc.tensor.matmul_mx(
                out=acc[:],
                lhsT=uw[:, 0, 2 * P * t : 2 * P * (t + 1)].bitcast(FP4X4),
                lhsT_scale=us[:, 0, P * t : P * (t + 1)],
                rhs=d_codes[b][:].bitcast(FP8X4),
                rhs_scale=d_scl[b][:],
                start=True,
                stop=True,
            )
            nc.scalar.activation(
                out=q_planes[b][:, t, :], in_=acc[:], func=ACT.Identity, bias=bias[:, t : t + 1], scale=1.0
            )

        def q_weave(b, half):
            cols = slice(HALF * half, HALF * (half + 1))
            nc.vector.tensor_copy(
                out=q_grp[b][:, cols, :].rearrange("p (c w) t -> p c t w", w=4),
                in_=q_planes[b][:, :, cols].rearrange("p t (c w) -> p c t w", w=4),
            )

        def s_matmul(b, i):
            acc = bank("s", [P, S], F32)
            scores[(b, i)] = acc
            cols = slice(P * i, P * (i + 1))
            nc.tensor.matmul_mx(
                out=acc[:],
                lhsT=q_codes[b][:, cols].bitcast(FP8X4),
                lhsT_scale=q_scl[b][:, cols],
                rhs=h_codes[b][:].bitcast(FP8X4),
                rhs_scale=h_scl[b][:],
                start=True,
                stop=True,
            )

        def row_stats(b, i):
            n = TILES * b + i
            nc.vector.tensor_scalar(
                out=neg_s[n][:],
                in0=scores[(b, i)][:],
                scalar1=-1.0 / math.sqrt(D),
                scalar2=None,
                op0=ALU.mult,
                op1=ALU.min,
                accum_out=neg_max[b][:, i : i + 1],
            )
            nc.scalar.activation(
                out=exp_out[i % 2][:],
                in_=neg_s[n][:],
                func=ACT.Exp,
                bias=neg_max[b][:, i : i + 1],
                scale=-1.0,
                accum_out=sums[b][:, i : i + 1],
            )

        def row_log(b):
            nc.scalar.activation(out=logs[b][:], in_=sums[b][:], func=ACT.Ln)

        def store(b, i):
            nc.sync.dma_start(out=out[b].rearrange("(p i) n -> i p n", i=TILES)[i], in_=res[TILES * b + i][:])

        def finish_first(i, engine):
            engine.tensor_scalar(
                out=res[i][:], in0=neg_s[i][:], scalar1=-1.0, scalar2=shift[:, i : i + 1], op0=ALU.mult, op1=ALU.add
            )
            store(0, i)

        def centre_last(i):
            nc.vector.tensor_scalar(
                out=res[TILES + i][:],
                in0=neg_s[TILES + i][:],
                scalar1=neg_max[1][:, i : i + 1],
                scalar2=-1.0,
                op0=ALU.subtract,
                op1=ALU.mult,
            )

        def finish_last(i):
            nc.vector.tensor_scalar(
                out=res[TILES + i][:],
                in0=res[TILES + i][:],
                scalar1=logs[1][:, i : i + 1],
                scalar2=None,
                op0=ALU.subtract,
            )
            store(1, i)


        for g in range(E_PASSES):
            spread_scale(g)
        for g in range(E_PASSES):
            scale_e(0, slice(K_PASS * g, K_PASS * (g + 1)))
        turn_d(0, 0)
        turn_d(0, 1)
        scale_e(1)
        turn_e(0)
        scale_e(2)
        turn_e(1)
        turn_d(1, 0)
        scale_e(3)
        quant_d(0)
        turn_e(2)
        reorder(uw, uw_raw)
        reorder(us, us_raw)
        turn_e(3)
        turn_d(1, 1)

        turn_bias()
        for t in range(SLOTS):
            q_plane(0, t)
        scale_e(TILES)
        reorder(ww, ww_raw)
        reorder(ws, ws_raw)
        quant_e(0)
        turn_e(TILES)
        for t in range(SLOTS):
            z_plane(0, t)
        for n in range(TILES + 1, B * TILES):
            scale_e(n)
        for n in range(TILES + 1, B * TILES):
            turn_e(n)

        quant_d(1)
        q_weave(0, 0)
        q_weave(0, 1)
        leaky(0, 0)
        quant_q(0, 0)
        quant_e(1)
        for t in range(SLOTS):
            q_plane(1, t)
        leaky(0, 1)
        quant_q(0, 1)
        quant_h(0)

        for t in range(SLOTS - 1):
            z_plane(1, t)
        s_matmul(0, 0)
        s_matmul(0, 1)
        z_plane(1, SLOTS - 1)
        s_matmul(0, 2)
        s_matmul(0, 3)
        q_weave(1, 0)
        for i in range(TILES):
            row_stats(0, i)

        row_log(0)
        leaky(1, 0)
        leaky(1, 1)
        quant_q(1, 0)
        quant_h(1)
        s_matmul(1, 0)
        s_matmul(1, 1)
        q_weave(1, 1)
        quant_q(1, 1)
        s_matmul(1, 2)
        s_matmul(1, 3)

        nc.vector.tensor_tensor(out=shift[:], in0=neg_max[0][:], in1=logs[0][:], op=ALU.subtract)
        for i in range(TILES // 2):
            finish_first(i, nc.gpsimd)
        for i in range(TILES):
            row_stats(1, i)

        row_log(1)
        for i in range(TILES // 2, TILES):
            finish_first(i, nc.vector)
        for i in range(TILES):
            centre_last(i)
        for i in range(TILES):
            finish_last(i)
